import numpy as np
import ml_dtypes


def mxq(x, axis, fmt="e4m3"):
    dtype, down = {"e4m3": (ml_dtypes.float8_e4m3fn, 7), "e5m2": (ml_dtypes.float8_e5m2, 14)}[fmt]
    v = np.moveaxis(np.asarray(x, np.float32).astype(ml_dtypes.bfloat16).astype(np.float64), axis, -1)
    blocks = v.reshape(v.shape[:-1] + (-1, 32))
    amax = np.abs(blocks).max(-1, keepdims=True)
    byte = np.maximum(np.where(amax > 0, np.frexp(amax)[1] - 1 + 127, 0) - down, 1)
    scale = np.exp2(byte - 127.0)
    codes = (blocks / scale).astype(np.float32).astype(dtype).astype(np.float64)
    return np.moveaxis((codes * scale).reshape(v.shape), -1, axis)


WIDE = False


def mx_kscale(k):
    if not WIDE:
        return np.ones(k)
    levels = np.array([10, -10, 5, -5, 0])
    if k % 512:
        return np.exp2(np.random.permutation(np.resize(levels, k // 32))).repeat(32)
    a = np.empty((k // 512, 16))
    for p in range(k // 512):
        a[p, :8] = np.random.permutation(np.resize(levels, 8))
        for g in range(8):
            far = levels[np.abs(levels - a[p, g]) >= 10]
            a[p, g + 8] = far[np.random.randint(len(far))]
    return np.exp2(a.ravel()).repeat(32)


def f64(x):
    return np.asarray(x).astype(np.float64)


def striped(idx):
    return np.tile(idx.reshape(-1, 16).T, (8, 1)).astype(np.uint16)


def unstriped(offs):
    return offs[:16].T.reshape(-1).astype(np.int64)


def pack_weight(w):
    k, n = w.shape
    w = f64(np.asarray(w, np.float32).astype(ml_dtypes.bfloat16)).reshape(k // 32, 32, n)
    amax = np.abs(w).max(1)
    byte = np.clip(np.where(amax > 0, np.frexp(amax)[1] - 1 + 127 - 7, 1), 1, 254)
    scaled = (w * np.exp2(127.0 - byte)[:, None, :]).reshape(k, n).astype(np.float32)
    words = np.ascontiguousarray(scaled.reshape(k // 512, 128, 4, n).transpose(0, 1, 3, 2)).astype(ml_dtypes.float8_e4m3fn).view(np.uint8)
    return words, np.ascontiguousarray(byte.astype(np.uint8).reshape(k // 512, 16, n))


def unpack_weight(words, scales):
    g, p, n, _ = words.shape
    vals = np.ascontiguousarray(words).view(ml_dtypes.float8_e4m3fn).astype(np.float64) * np.repeat(np.exp2(scales.astype(np.float64) - 127.0), 8, axis=1)[..., None]
    return vals.transpose(0, 1, 3, 2).reshape(g * 512, n)


K, T, S, N, H, W, U = 512, 1024, 512, 256, 512, 2048, 1024


def setup_inputs():
    n = np.random.standard_normal
    s = mx_kscale(K)[:, None]
    u = mx_kscale(H)
    packed_xT = pack_weight(n((K, T)) * s)
    packed_eT = pack_weight(n((K, W)) * s)
    return {
        "x_words": packed_xT[0],
        "x_scales": packed_xT[1],
        "w1": (n((K, H)) / np.sqrt(K) / s).astype(np.float32),
        "e_words": packed_eT[0],
        "e_scales": packed_eT[1],
        "w2": (n((K, H)) / np.sqrt(K) / s).astype(np.float32),
        "unit": (np.random.uniform(0.6, 1.4, (H, 1)) * u[:, None]).astype(np.float32),
        "w3": (n((H, N)) / np.sqrt(H) / u[:, None]).astype(np.float32),
        "offs": striped(np.random.permutation(T)[:S]),
        "doc": striped(np.random.permutation(W)[:S]),
        "qa": striped(np.random.permutation(np.concatenate([np.arange(S), np.random.randint(0, S, U - S)]))),
        "qb": striped(np.random.permutation(np.concatenate([np.arange(S), np.random.randint(0, S, U - S)]))),
        "da": striped(np.random.permutation(np.concatenate([np.arange(S), np.random.randint(0, S, U - S)]))),
        "db": striped(np.random.permutation(np.concatenate([np.arange(S), np.random.randint(0, S, U - S)]))),
    }


def reference(x_words, x_scales, w1, e_words, e_scales, w2, unit, w3, offs, doc, qa, qb, da, db):
    xq = unpack_weight(x_words, x_scales)[:, unstriped(offs)]
    y = mxq(f64(w1), 0, "e4m3").T @ xq
    y_1 = y[:, unstriped(qa)]
    e_doc = unpack_weight(e_words, e_scales)[:, unstriped(doc)]
    ye = mxq(f64(w2), 0, "e4m3").T @ e_doc
    e_1 = ye[:, unstriped(da)]
    sumq = y_1 + e_1
    y_2 = y[:, unstriped(qb)]
    e_2 = ye[:, unstriped(db)]
    difq = y_2 - e_2
    hid = f64(unit) * (sumq * difq)
    return mxq(f64(w3), 0, "e4m3").T @ mxq(hid, 0, "e4m3")

@@ -1,0 +1,157 @@
+from contextlib import ExitStack
+
+import concourse.mybir as mybir
+
+K, T, S, N, H, W, U = 512, 1024, 512, 256, 512, 2048, 1024
+FLOPS = 2 * K * H * S * 2 + 2 * H * N * U
+
+F32 = mybir.dt.float32
+BF16 = mybir.dt.bfloat16
+I32 = mybir.dt.int32
+U32 = mybir.dt.uint32
+U16 = mybir.dt.uint16
+U8 = mybir.dt.uint8
+FP8X4 = mybir.dt.float8_e4m3fn_x4
+COPY = mybir.ActivationFunctionType.Copy
+MULT = mybir.AluOpType.mult
+ADD = mybir.AluOpType.add
+
+P = 128
+PACK = 4
+WINDOW = S + 8
+CHUNKS = (512, 256, 256)
+
+
+def tile_picked_ydocqa_bil_p_kernel(tc, x_words, x_scales, w1, e_words, e_scales, w2, unit, w3, offs, doc, qa, qb, da, db, out):
+    nc = tc.nc
+    with ExitStack() as ctx:
+        lists = ctx.enter_context(tc.tile_pool(name="lists", bufs=1))
+        keep = ctx.enter_context(tc.tile_pool(name="keep", bufs=1))
+        psum = ctx.enter_context(tc.psum_pool(name="psum", bufs=8))
+
+        def load_list(name, src):
+            tile = lists.tile(list(src.shape), U16, name=name)
+            nc.sync.dma_start(tile[:], src)
+            return tile
+
+        def load_words(name, src):
+            tile = keep.tile([P, src.shape[2]], U32, name=name)
+            nc.sync.dma_start(tile[:].bitcast(I32), src[0].rearrange("p n t -> p (n t)").bitcast(I32))
+            return tile
+
+        def load_scales(name, src, clear, queue):
+            tile = keep.tile([P, src.shape[2]], U8, name=name)
+            clear.memset(tile[:].bitcast(I32), 0)
+            for q in range(4):
+                queue.dma_start(tile[32 * q : 32 * q + 4, :].bitcast(I32), src[0, 4 * q : 4 * q + 4, :].bitcast(I32))
+            return tile
+
+        def load_weight(name, src, cols):
+            tile = keep.tile([P, PACK, cols.stop - cols.start], F32, name=name)
+            nc.sync.dma_start(tile[:], src.rearrange("(p j) c -> p j c", j=PACK)[:, :, cols])
+            return tile
+
+        halves = (slice(0, H // 2), slice(H // 2, H))
+        offs_t = load_list("offs_t", offs)
+        xw = load_words("xw", x_words)
+        xs = load_scales("xs", x_scales, nc.gpsimd, nc.gpsimd)
+        unit_t = keep.tile([P, PACK], F32, name="unit_t")
+        nc.gpsimd.dma_start(unit_t[:], unit.rearrange("(p t) o -> p (t o)", t=PACK))
+        w1_raw = [load_weight("w1_raw%d" % h, w1, halves[h]) for h in range(2)]
+        doc_t = load_list("doc_t", doc)
+        qa_t = load_list("qa_t", qa)
+        qb_t = load_list("qb_t", qb)
+        ew = load_words("ew", e_words)
+        es = load_scales("es", e_scales, nc.vector, nc.sync)
+        w2_raw = [load_weight("w2_raw%d" % h, w2, halves[h]) for h in range(2)]
+        da_t = load_list("da_t", da)
+        db_t = load_list("db_t", db)
+        w3_raw = load_weight("w3_raw", w3, slice(0, N))
+
+        def pick(name, words, scales, offsets):
+            codes = keep.tile([P, S], U32, name=name + "_codes", align_bytes=64)
+            plane = keep.tile([P, S], U8, name=name + "_plane", align_bytes=64)
+            nc.vector.tensor_copy(codes[:], words[:].indirect(offsets[:]))
+            nc.vector.tensor_copy(plane[:], scales[:].indirect(offsets[:]))
+            return codes, plane
+
+        def quantise_dealt(name, raw):
+            grouped = keep.tile([P, PACK * H], BF16, name=name + "_grouped", align_bytes=64)
+            dealt = grouped[:].rearrange("p (t m j) -> p m j t", t=PACK, j=PACK)
+            m_half = P // 2
+            nc.scalar.copy(dealt[:, :m_half], raw[0][:].rearrange("p j (m t) -> p m j t", t=PACK))
+            nc.vector.tensor_copy(dealt[:, m_half:], raw[1][:].rearrange("p j (m t) -> p m j t", t=PACK))
+            codes = keep.tile([P, H], U32, name=name + "_codes", align_bytes=64)
+            plane = keep.tile([P, H], U8, name=name + "_plane", align_bytes=64)
+            for half in halves:
+                nc.vector.quantize_mx(codes[:, half].bitcast(FP8X4), plane[:, half], grouped[:, PACK * half.start : PACK * half.stop])
+            return codes, plane
+
+        def product(lhs, cols, rhs, width):
+            acc = psum.tile([P, 512], F32, name="acc")
+            nc.tensor.matmul_mx(
+                acc[:, :width], lhsT=lhs[0][:, cols].bitcast(FP8X4), lhsT_scale=lhs[1][:, cols],
+                rhs=rhs[0][:].bitcast(FP8X4), rhs_scale=rhs[1][:], start=True, stop=True)
+            return acc
+
+        def window(name):
+            return keep.tile([P, WINDOW], F32, name=name)
+
+        xq = pick("x", xw, xs, offs_t)
+        w1q = quantise_dealt("w1", w1_raw)
+        y, uy = [], []
+        for t in range(PACK):
+            acc = product(w1q, slice(t * P, (t + 1) * P), xq, S)
+            y.append(window("y%d" % t))
+            nc.scalar.copy(y[t][:, :S], acc[:])
+            uy.append(window("uy%d" % t))
+            nc.gpsimd.tensor_scalar(uy[t][:, :S], y[t][:, :S], unit_t[:, t : t + 1], 0.0, MULT, ADD)
+
+        eq = pick("e", ew, es, doc_t)
+        w2q = quantise_dealt("w2", w2_raw)
+        ne, ue = [], []
+        for t in range(PACK):
+            acc = product(w2q, slice(t * P, (t + 1) * P), eq, S)
+            ne.append(window("ne%d" % t))
+            nc.scalar.activation(ne[t][:, :S], acc[:], COPY, scale=-1.0)
+            ue.append(window("ue%d" % t))
+            nc.vector.tensor_scalar(ue[t][:, :S], ne[t][:, :S], unit_t[:, t : t + 1], -1.0, MULT, MULT)
+
+        w3_grouped = keep.tile([P, PACK * N], BF16, name="w3_grouped", align_bytes=64)
+        w3_codes = keep.tile([P, N], U32, name="w3_codes", align_bytes=64)
+        w3_plane = keep.tile([P, N], U8, name="w3_plane", align_bytes=64)
+
+        start = 0
+        for c, width in enumerate(CHUNKS):
+            cols = slice(start // 16, (start + width) // 16)
+            sums = keep.tile([P, PACK, width], F32, name="sums%d" % c)
+            difs = keep.tile([P, PACK, width], F32, name="difs%d" % c)
+            for t in range(PACK):
+                y2 = keep.tile([P, width], F32, name="y2_%d_%d" % (c, t))
+                nc.scalar.activation(y2[:], y[t][:].indirect(qb_t[:, cols]), COPY)
+                y1 = keep.tile([P, width], F32, name="y1_%d_%d" % (c, t))
+                nc.scalar.activation(y1[:], uy[t][:].indirect(qa_t[:, cols]), COPY)
+                nc.vector.tensor_tensor(difs[:, t, :], ne[t][:].indirect(db_t[:, cols]), y2[:], ADD)
+                nc.vector.tensor_tensor(sums[:, t, :], ue[t][:].indirect(da_t[:, cols]), y1[:], ADD)
+            if c == 0:
+                nc.scalar.copy(
+                    w3_grouped[:].rearrange("p (c i j) -> p c j i", i=4, j=PACK),
+                    w3_raw[:].rearrange("p j (c i) -> p c j i", i=4))
+                nc.vector.quantize_mx(w3_codes[:].bitcast(FP8X4), w3_plane[:], w3_grouped[:])
+            hid = keep.tile([P, PACK * width], BF16, name="hid%d" % c, align_bytes=64)
+            nc.vector.tensor_tensor(
+                hid[:].rearrange("p (c i t) -> p c t i", i=4, t=PACK),
+                sums[:].rearrange("p t (c i) -> p c t i", i=4),
+                difs[:].rearrange("p t (c i) -> p c t i", i=4), MULT)
+            hid_codes = keep.tile([P, width], U32, name="hid_codes%d" % c, align_bytes=64)
+            hid_plane = keep.tile([P, width], U8, name="hid_plane%d" % c, align_bytes=64)
+            nc.vector.quantize_mx(hid_codes[:].bitcast(FP8X4), hid_plane[:], hid[:])
+            for h in range(N // P):
+                acc = product((w3_codes, w3_plane), slice(h * P, (h + 1) * P), (hid_codes, hid_plane), width)
+                staged = keep.tile([P, width], F32, name="staged%d_%d" % (c, h))
+                if c == len(CHUNKS) - 1 and h == 1:
+                    nc.vector.tensor_copy(staged[:], acc[:, :width])
+                else:
+                    nc.scalar.copy(staged[:], acc[:, :width])
+                nc.sync.dma_start(out[h * P : (h + 1) * P, start : start + width], staged[:])
+            start += width

@@ -13,13 +13,28 @@ U16 = mybir.dt.uint16
 U8 = mybir.dt.uint8
 FP8X4 = mybir.dt.float8_e4m3fn_x4
 COPY = mybir.ActivationFunctionType.Copy
+RSQRT = mybir.ActivationFunctionType.Abs_reciprocal_sqrt
 MULT = mybir.AluOpType.mult
 ADD = mybir.AluOpType.add
+MIN = mybir.AluOpType.min
+IS_LT = mybir.AluOpType.is_lt
 
 P = 128
 PACK = 4
-WINDOW = S + 8
-CHUNKS = (512, 256, 256)
+BANK = 512
+CHUNKS = (512, 384, 128)
+WINDOW = U + 8
+BOTH_ON_SCALAR = ((1, 0), (1, 1), (2, 0), (2, 1))
+TINY = 2.0 ** -120
+
+
+def pieces(width, sizes):
+    parts, start = [], 0
+    while start < width:
+        size = max(s for s in sizes if s <= width - start)
+        parts.append(slice(start, start + size))
+        start += size
+    return parts
 
 
 def tile_picked_ydocqa_bil_p_kernel(tc, x_words, x_scales, w1, e_words, e_scales, w2, unit, w3, offs, doc, qa, qb, da, db, out):
@@ -27,6 +42,7 @@ def tile_picked_ydocqa_bil_p_kernel(tc, x_words, x_scales, w1, e_words, e_scales
     with ExitStack() as ctx:
         lists = ctx.enter_context(tc.tile_pool(name="lists", bufs=1))
         keep = ctx.enter_context(tc.tile_pool(name="keep", bufs=1))
+        ring = ctx.enter_context(tc.tile_pool(name="ring", bufs=4))
         psum = ctx.enter_context(tc.psum_pool(name="psum", bufs=8))
 
         def load_list(name, src):
@@ -39,11 +55,18 @@ def tile_picked_ydocqa_bil_p_kernel(tc, x_words, x_scales, w1, e_words, e_scales
             nc.sync.dma_start(tile[:].bitcast(I32), src[0].rearrange("p n t -> p (n t)").bitcast(I32))
             return tile
 
-        def load_scales(name, src, clear, queue):
+        def load_scales(name, src):
             tile = keep.tile([P, src.shape[2]], U8, name=name)
-            clear.memset(tile[:].bitcast(I32), 0)
+            nc.vector.memset(tile[:].bitcast(I32), 0)
             for q in range(4):
-                queue.dma_start(tile[32 * q : 32 * q + 4, :].bitcast(I32), src[0, 4 * q : 4 * q + 4, :].bitcast(I32))
+                nc.sync.dma_start(tile[32 * q : 32 * q + 4, :].bitcast(I32), src[0, 4 * q : 4 * q + 4, :].bitcast(I32))
+            return tile
+
+        def load_scales_repeated(name, src):
+            tile = keep.tile([P, src.shape[2]], U8, name=name)
+            n = src.shape[2] // 4
+            for q in range(4):
+                nc.sync.dma_start(tile[32 * q : 32 * q + 32, :].bitcast(I32), src[0, 4 * q : 4 * q + 4, :].bitcast(I32).unsqueeze(0).to_broadcast([8, 4, n]))
             return tile
 
         def load_weight(name, src, cols):
@@ -52,106 +75,165 @@ def tile_picked_ydocqa_bil_p_kernel(tc, x_words, x_scales, w1, e_words, e_scales
             return tile
 
         halves = (slice(0, H // 2), slice(H // 2, H))
+        unit_t = keep.tile([P, PACK], F32, name="unit_t")
+        nc.sync.dma_start(unit_t[:], unit.rearrange("(p t) o -> p (t o)", t=PACK))
         offs_t = load_list("offs_t", offs)
         xw = load_words("xw", x_words)
-        xs = load_scales("xs", x_scales, nc.gpsimd, nc.gpsimd)
-        unit_t = keep.tile([P, PACK], F32, name="unit_t")
-        nc.gpsimd.dma_start(unit_t[:], unit.rearrange("(p t) o -> p (t o)", t=PACK))
+        xs = load_scales_repeated("xs", x_scales)
         w1_raw = [load_weight("w1_raw%d" % h, w1, halves[h]) for h in range(2)]
         doc_t = load_list("doc_t", doc)
-        qa_t = load_list("qa_t", qa)
+        es = load_scales("es", e_scales)
+        w2_raw = [load_weight("w2_raw%d" % h, w2, halves[h]) for h in range(2)]
         qb_t = load_list("qb_t", qb)
         ew = load_words("ew", e_words)
-        es = load_scales("es", e_scales, nc.vector, nc.sync)
-        w2_raw = [load_weight("w2_raw%d" % h, w2, halves[h]) for h in range(2)]
-        da_t = load_list("da_t", da)
+        qa_t = load_list("qa_t", qa)
         db_t = load_list("db_t", db)
+        da_t = load_list("da_t", da)
         w3_raw = load_weight("w3_raw", w3, slice(0, N))
 
-        def pick(name, words, scales, offsets):
-            codes = keep.tile([P, S], U32, name=name + "_codes", align_bytes=64)
-            plane = keep.tile([P, S], U8, name=name + "_plane", align_bytes=64)
-            nc.vector.tensor_copy(codes[:], words[:].indirect(offsets[:]))
-            nc.vector.tensor_copy(plane[:], scales[:].indirect(offsets[:]))
-            return codes, plane
+        def small(name):
+            return keep.tile([P, PACK], F32, name=name)
 
-        def quantise_dealt(name, raw):
-            grouped = keep.tile([P, PACK * H], BF16, name=name + "_grouped", align_bytes=64)
+        twice_neg, flip, neg_abs, clamped, guess = small("twice_neg"), small("flip"), small("neg_abs"), small("clamped"), small("guess")
+        nc.vector.scalar_tensor_tensor(neg_abs[:], unit_t[:], -1.0, unit_t[:], MULT, MIN)
+        nc.vector.tensor_scalar(clamped[:], neg_abs[:], -TINY, None, MIN)
+        nc.scalar.activation(guess[:], clamped[:], RSQRT)
+        rough, err, corr = small("rough"), small("err"), small("corr")
+        nc.gpsimd.tensor_tensor(rough[:], guess[:], neg_abs[:], MULT)
+        nc.gpsimd.tensor_tensor(err[:], rough[:], guess[:], MULT)
+        nc.gpsimd.tensor_scalar(corr[:], err[:], 0.5, 1.5, MULT, ADD)
+        nc.gpsimd.tensor_scalar(twice_neg[:], unit_t[:], 0.0, 2.0, IS_LT, MULT)
+        nc.gpsimd.tensor_scalar(flip[:], twice_neg[:], 1.0, -1.0, MULT, ADD)
+
+        def ring_tile(shape, dtype, name):
+            return ring.tile(shape, dtype, name=name, tag="ring", align_bytes=64)
+
+        root = {}
+
+        def root_column(t, in_ring):
+            root[t] = staged_tile(in_ring, [P, 1], F32, "root%d" % t)
+            nc.gpsimd.tensor_tensor(root[t][:], corr[:, t : t + 1], rough[:, t : t + 1], MULT)
+
+        def staged_tile(in_ring, shape, dtype, name):
+            if in_ring:
+                return ring_tile(shape, dtype, name)
+            return keep.tile(shape, dtype, name=name, align_bytes=64)
+
+        def pick(name, table, dtype, offsets, in_ring):
+            if name == "e_plane":
+                picked = keep.tile([P, S], dtype, name=name, tag="w1_grouped", align_bytes=64)
+            else:
+                picked = staged_tile(in_ring, [P, S], dtype, name)
+            nc.vector.tensor_copy(picked[:], table[:].indirect(offsets[:]))
+            return picked
+
+        def quantise_dealt(name, raw, shares):
+            grouped = keep.tile([P, PACK * H], BF16, name=name + "_grouped", tag=name + "_grouped", align_bytes=64)
             dealt = grouped[:].rearrange("p (t m j) -> p m j t", t=PACK, j=PACK)
-            m_half = P // 2
-            nc.scalar.copy(dealt[:, :m_half], raw[0][:].rearrange("p j (m t) -> p m j t", t=PACK))
-            nc.vector.tensor_copy(dealt[:, m_half:], raw[1][:].rearrange("p j (m t) -> p m j t", t=PACK))
-            codes = keep.tile([P, H], U32, name=name + "_codes", align_bytes=64)
-            plane = keep.tile([P, H], U8, name=name + "_plane", align_bytes=64)
-            for half in halves:
-                nc.vector.quantize_mx(codes[:, half].bitcast(FP8X4), plane[:, half], grouped[:, PACK * half.start : PACK * half.stop])
-            return codes, plane
+            for engine, lo, hi in shares:
+                h = lo // 64
+                src = raw[h][:].rearrange("p j (m t) -> p m j t", t=PACK)[:, lo - 64 * h : hi - 64 * h]
+                if engine == "scalar":
+                    nc.scalar.copy(dealt[:, lo:hi], src)
+                else:
+                    nc.vector.tensor_copy(dealt[:, lo:hi], src)
+            return grouped
 
-        def product(lhs, cols, rhs, width):
-            acc = psum.tile([P, 512], F32, name="acc")
-            nc.tensor.matmul_mx(
-                acc[:, :width], lhsT=lhs[0][:, cols].bitcast(FP8X4), lhsT_scale=lhs[1][:, cols],
-                rhs=rhs[0][:].bitcast(FP8X4), rhs_scale=rhs[1][:], start=True, stop=True)
+        def quantise_tiles(name, grouped, first, count, in_ring):
+            codes = staged_tile(in_ring, [P, count * P], U32, "%s_codes%d" % (name, first))
+            plane = staged_tile(in_ring, [P, count * P], U8, "%s_plane%d" % (name, first))
+            nc.vector.quantize_mx(codes[:].bitcast(FP8X4), plane[:], grouped[:, PACK * P * first : PACK * P * (first + count)])
+            return [(codes[:, i * P : (i + 1) * P], plane[:, i * P : (i + 1) * P]) for i in range(count)]
+
+        def product(lhs, rhs, width):
+            acc = psum.tile([P, BANK], F32, name="acc")
+            for part in pieces(width, (512, 256, 128)):
+                nc.tensor.matmul_mx(
+                    acc[:, part], lhsT=lhs[0].bitcast(FP8X4), lhsT_scale=lhs[1],
+                    rhs=rhs[0][:, part].bitcast(FP8X4), rhs_scale=rhs[1][:, part], start=True, stop=True)
             return acc
 
-        def window(name):
-            return keep.tile([P, WINDOW], F32, name=name)
+        def window(name, t, acc, engine):
+            tile = keep.tile([P, WINDOW], F32, name="%s%d" % (name, t))
+            if engine == "scalar":
+                nc.scalar.activation(tile[:, :S], acc[:], COPY, scale=root[t][:])
+            else:
+                nc.vector.tensor_scalar(tile[:, :S], acc[:], root[t][:], None, MULT)
+            return tile
 
-        xq = pick("x", xw, xs, offs_t)
-        w1q = quantise_dealt("w1", w1_raw)
-        y, uy = [], []
-        for t in range(PACK):
-            acc = product(w1q, slice(t * P, (t + 1) * P), xq, S)
-            y.append(window("y%d" % t))
-            nc.scalar.copy(y[t][:, :S], acc[:])
-            uy.append(window("uy%d" % t))
-            nc.gpsimd.tensor_scalar(uy[t][:, :S], y[t][:, :S], unit_t[:, t : t + 1], 0.0, MULT, ADD)
+        def fetch(tile, offsets, width, sign):
+            part = ring_tile([P, width], F32, "part")
+            nc.scalar.activation(part[:], tile[:].indirect(offsets), COPY, scale=sign)
+            return part
 
-        eq = pick("e", ew, es, doc_t)
-        w2q = quantise_dealt("w2", w2_raw)
-        ne, ue = [], []
-        for t in range(PACK):
-            acc = product(w2q, slice(t * P, (t + 1) * P), eq, S)
-            ne.append(window("ne%d" % t))
-            nc.scalar.activation(ne[t][:, :S], acc[:], COPY, scale=-1.0)
-            ue.append(window("ue%d" % t))
-            nc.vector.tensor_scalar(ue[t][:, :S], ne[t][:, :S], unit_t[:, t : t + 1], -1.0, MULT, MULT)
+        root_column(0, True)
+        root_column(1, True)
+        x_codes = pick("x_codes", xw, U32, offs_t, False)
+        x_plane = pick("x_plane", xs, U8, offs_t, False)
+        w1_grouped = quantise_dealt("w1", w1_raw, (("scalar", 0, 64), ("vector", 64, 104), ("scalar", 104, 128)))
+        w1q = quantise_tiles("w1", w1_grouped, 0, 1, False) + quantise_tiles("w1", w1_grouped, 1, 3, False)
+        y_acc = [product(w1q[t], (x_codes, x_plane), S) for t in range(PACK)]
+        w2_grouped = quantise_dealt("w2", w2_raw, (("vector", 0, 64), ("vector", 64, 128)))
+        w2q = quantise_tiles("w2", w2_grouped, 0, 1, False)
+        e_plane = pick("e_plane", es, U8, doc_t, False)
+        e_codes = pick("e_codes", ew, U32, doc_t, False)
+        w2q = w2q + quantise_tiles("w2", w2_grouped, 1, 3, False)
+        e_acc = [product(w2q[t], (e_codes, e_plane), S) for t in range(PACK)]
 
-        w3_grouped = keep.tile([P, PACK * N], BF16, name="w3_grouped", align_bytes=64)
+        w3_grouped = keep.tile([P, PACK * N], BF16, name="w3_grouped", tag="pairs", align_bytes=64)
         w3_codes = keep.tile([P, N], U32, name="w3_codes", align_bytes=64)
         w3_plane = keep.tile([P, N], U8, name="w3_plane", align_bytes=64)
+        nc.vector.tensor_tensor(
+            w3_grouped[:].rearrange("p (c i j) -> p c j i", i=4, j=PACK),
+            w3_raw[:].rearrange("p j (c i) -> p c j i", i=4),
+            flip[:].unsqueeze(1).unsqueeze(3).to_broadcast([P, N // 4, PACK, 4]), MULT)
+        nc.vector.quantize_mx(w3_codes[:].bitcast(FP8X4), w3_plane[:], w3_grouped[:])
 
+        pairs = keep.tile([P, 2, PACK, U], F32, name="pairs", tag="pairs", align_bytes=64)
+        pair = [pairs[:, s] for s in range(2)]
+        sides = ((qb_t, db_t, -1.0), (qa_t, da_t, 1.0))
+        y_engine = ("scalar", "scalar", "scalar", "scalar")
+        y = {0: window("y", 0, y_acc[0], y_engine[0])}
+        e = {}
+        first_part = fetch(y[0], qb_t[:], U, -1.0)
+        root_column(2, True)
+        root_column(3, False)
+        for t in range(PACK - 1):
+            e[t] = window("e", t, e_acc[t], "scalar")
+
+            for s, (q_list, d_list, sign) in enumerate(sides):
+                y_part = first_part if (t, s) == (0, 0) else fetch(y[t], q_list[:], U, sign)
+                nc.vector.tensor_tensor(pair[s][:, t, :], e[t][:].indirect(d_list[:]), y_part[:], ADD)
+            y[t + 1] = window("y", t + 1, y_acc[t + 1], y_engine[t + 1])
+
+        last = PACK - 1
+        e[last] = window("e", last, e_acc[last], "scalar")
         start = 0
         for c, width in enumerate(CHUNKS):
             cols = slice(start // 16, (start + width) // 16)
-            sums = keep.tile([P, PACK, width], F32, name="sums%d" % c)
-            difs = keep.tile([P, PACK, width], F32, name="difs%d" % c)
-            for t in range(PACK):
-                y2 = keep.tile([P, width], F32, name="y2_%d_%d" % (c, t))
-                nc.scalar.activation(y2[:], y[t][:].indirect(qb_t[:, cols]), COPY)
-                y1 = keep.tile([P, width], F32, name="y1_%d_%d" % (c, t))
-                nc.scalar.activation(y1[:], uy[t][:].indirect(qa_t[:, cols]), COPY)
-                nc.vector.tensor_tensor(difs[:, t, :], ne[t][:].indirect(db_t[:, cols]), y2[:], ADD)
-                nc.vector.tensor_tensor(sums[:, t, :], ue[t][:].indirect(da_t[:, cols]), y1[:], ADD)
-            if c == 0:
-                nc.scalar.copy(
-                    w3_grouped[:].rearrange("p (c i j) -> p c j i", i=4, j=PACK),
-                    w3_raw[:].rearrange("p j (c i) -> p c j i", i=4))
-                nc.vector.quantize_mx(w3_codes[:].bitcast(FP8X4), w3_plane[:], w3_grouped[:])
+            span = slice(start, start + width)
+            for s, (q_list, d_list, sign) in enumerate(sides):
+                y_part = fetch(y[last], q_list[:, cols], width, sign)
+                if (c, s) in BOTH_ON_SCALAR:
+                    e_part = fetch(e[last], d_list[:, cols], width, 1.0)
+                    nc.vector.tensor_tensor(pair[s][:, last, span], e_part[:], y_part[:], ADD)
+                else:
+                    nc.vector.tensor_tensor(pair[s][:, last, span], e[last][:].indirect(d_list[:, cols]), y_part[:], ADD)
             hid = keep.tile([P, PACK * width], BF16, name="hid%d" % c, align_bytes=64)
             nc.vector.tensor_tensor(
                 hid[:].rearrange("p (c i t) -> p c t i", i=4, t=PACK),
-                sums[:].rearrange("p t (c i) -> p c t i", i=4),
-                difs[:].rearrange("p t (c i) -> p c t i", i=4), MULT)
+                pair[0][:, :, span].rearrange("p t (c i) -> p c t i", i=4),
+                pair[1][:, :, span].rearrange("p t (c i) -> p c t i", i=4), MULT)
             hid_codes = keep.tile([P, width], U32, name="hid_codes%d" % c, align_bytes=64)
             hid_plane = keep.tile([P, width], U8, name="hid_plane%d" % c, align_bytes=64)
             nc.vector.quantize_mx(hid_codes[:].bitcast(FP8X4), hid_plane[:], hid[:])
             for h in range(N // P):
-                acc = product((w3_codes, w3_plane), slice(h * P, (h + 1) * P), (hid_codes, hid_plane), width)
                 staged = keep.tile([P, width], F32, name="staged%d_%d" % (c, h))
+                rows = slice(h * P, (h + 1) * P)
+                acc = product((w3_codes[:, rows], w3_plane[:, rows]), (hid_codes, hid_plane), width)
                 if c == len(CHUNKS) - 1 and h == 1:
                     nc.vector.tensor_copy(staged[:], acc[:, :width])
                 else:
                     nc.scalar.copy(staged[:], acc[:, :width])
-                nc.sync.dma_start(out[h * P : (h + 1) * P, start : start + width], staged[:])
+                nc.sync.dma_start(out[rows, span], staged[:])
             start += width

from contextlib import ExitStack

import concourse.mybir as mybir

K, T, S, N, H, W, U = 512, 1024, 512, 256, 512, 2048, 1024
FLOPS = 2 * K * H * S * 2 + 2 * H * N * U

F32 = mybir.dt.float32
BF16 = mybir.dt.bfloat16
I32 = mybir.dt.int32
U32 = mybir.dt.uint32
U16 = mybir.dt.uint16
U8 = mybir.dt.uint8
FP8X4 = mybir.dt.float8_e4m3fn_x4
COPY = mybir.ActivationFunctionType.Copy
RSQRT = mybir.ActivationFunctionType.Abs_reciprocal_sqrt
MULT = mybir.AluOpType.mult
ADD = mybir.AluOpType.add
MIN = mybir.AluOpType.min
IS_LT = mybir.AluOpType.is_lt

P = 128
PACK = 4
BANK = 512
CHUNKS = (512, 384, 128)
WINDOW = U + 8
BOTH_ON_SCALAR = ((1, 0), (1, 1), (2, 0), (2, 1))
TINY = 2.0 ** -120


def pieces(width, sizes):
    parts, start = [], 0
    while start < width:
        size = max(s for s in sizes if s <= width - start)
        parts.append(slice(start, start + size))
        start += size
    return parts


def tile_picked_ydocqa_bil_p_kernel(tc, x_words, x_scales, w1, e_words, e_scales, w2, unit, w3, offs, doc, qa, qb, da, db, out):
    nc = tc.nc
    with ExitStack() as ctx:
        lists = ctx.enter_context(tc.tile_pool(name="lists", bufs=1))
        keep = ctx.enter_context(tc.tile_pool(name="keep", bufs=1))
        ring = ctx.enter_context(tc.tile_pool(name="ring", bufs=4))
        psum = ctx.enter_context(tc.psum_pool(name="psum", bufs=8))

        def load_list(name, src):
            tile = lists.tile(list(src.shape), U16, name=name)
            nc.sync.dma_start(tile[:], src)
            return tile

        def load_words(name, src):
            tile = keep.tile([P, src.shape[2]], U32, name=name)
            nc.sync.dma_start(tile[:].bitcast(I32), src[0].rearrange("p n t -> p (n t)").bitcast(I32))
            return tile

        def load_scales(name, src):
            tile = keep.tile([P, src.shape[2]], U8, name=name)
            nc.vector.memset(tile[:].bitcast(I32), 0)
            for q in range(4):
                nc.sync.dma_start(tile[32 * q : 32 * q + 4, :].bitcast(I32), src[0, 4 * q : 4 * q + 4, :].bitcast(I32))
            return tile

        def load_scales_repeated(name, src):
            tile = keep.tile([P, src.shape[2]], U8, name=name)
            n = src.shape[2] // 4
            for q in range(4):
                nc.sync.dma_start(tile[32 * q : 32 * q + 32, :].bitcast(I32), src[0, 4 * q : 4 * q + 4, :].bitcast(I32).unsqueeze(0).to_broadcast([8, 4, n]))
            return tile

        def load_weight(name, src, cols):
            tile = keep.tile([P, PACK, cols.stop - cols.start], F32, name=name)
            nc.sync.dma_start(tile[:], src.rearrange("(p j) c -> p j c", j=PACK)[:, :, cols])
            return tile

        halves = (slice(0, H // 2), slice(H // 2, H))
        unit_t = keep.tile([P, PACK], F32, name="unit_t")
        nc.sync.dma_start(unit_t[:], unit.rearrange("(p t) o -> p (t o)", t=PACK))
        offs_t = load_list("offs_t", offs)
        xw = load_words("xw", x_words)
        xs = load_scales_repeated("xs", x_scales)
        w1_raw = [load_weight("w1_raw%d" % h, w1, halves[h]) for h in range(2)]
        doc_t = load_list("doc_t", doc)
        es = load_scales("es", e_scales)
        w2_raw = [load_weight("w2_raw%d" % h, w2, halves[h]) for h in range(2)]
        qb_t = load_list("qb_t", qb)
        ew = load_words("ew", e_words)
        qa_t = load_list("qa_t", qa)
        db_t = load_list("db_t", db)
        da_t = load_list("da_t", da)
        w3_raw = load_weight("w3_raw", w3, slice(0, N))

        def small(name):
            return keep.tile([P, PACK], F32, name=name)

        twice_neg, flip, neg_abs, clamped, guess = small("twice_neg"), small("flip"), small("neg_abs"), small("clamped"), small("guess")
        nc.vector.scalar_tensor_tensor(neg_abs[:], unit_t[:], -1.0, unit_t[:], MULT, MIN)
        nc.vector.tensor_scalar(clamped[:], neg_abs[:], -TINY, None, MIN)
        nc.scalar.activation(guess[:], clamped[:], RSQRT)
        rough, err, corr = small("rough"), small("err"), small("corr")
        nc.gpsimd.tensor_tensor(rough[:], guess[:], neg_abs[:], MULT)
        nc.gpsimd.tensor_tensor(err[:], rough[:], guess[:], MULT)
        nc.gpsimd.tensor_scalar(corr[:], err[:], 0.5, 1.5, MULT, ADD)
        nc.gpsimd.tensor_scalar(twice_neg[:], unit_t[:], 0.0, 2.0, IS_LT, MULT)
        nc.gpsimd.tensor_scalar(flip[:], twice_neg[:], 1.0, -1.0, MULT, ADD)

        def ring_tile(shape, dtype, name):
            return ring.tile(shape, dtype, name=name, tag="ring", align_bytes=64)

        root = {}

        def root_column(t, in_ring):
            root[t] = staged_tile(in_ring, [P, 1], F32, "root%d" % t)
            nc.gpsimd.tensor_tensor(root[t][:], corr[:, t : t + 1], rough[:, t : t + 1], MULT)

        def staged_tile(in_ring, shape, dtype, name):
            if in_ring:
                return ring_tile(shape, dtype, name)
            return keep.tile(shape, dtype, name=name, align_bytes=64)

        def pick(name, table, dtype, offsets, in_ring):
            if name == "e_plane":
                picked = keep.tile([P, S], dtype, name=name, tag="w1_grouped", align_bytes=64)
            else:
                picked = staged_tile(in_ring, [P, S], dtype, name)
            nc.vector.tensor_copy(picked[:], table[:].indirect(offsets[:]))
            return picked

        def quantise_dealt(name, raw, shares):
            grouped = keep.tile([P, PACK * H], BF16, name=name + "_grouped", tag=name + "_grouped", align_bytes=64)
            dealt = grouped[:].rearrange("p (t m j) -> p m j t", t=PACK, j=PACK)
            for engine, lo, hi in shares:
                h = lo // 64
                src = raw[h][:].rearrange("p j (m t) -> p m j t", t=PACK)[:, lo - 64 * h : hi - 64 * h]
                if engine == "scalar":
                    nc.scalar.copy(dealt[:, lo:hi], src)
                else:
                    nc.vector.tensor_copy(dealt[:, lo:hi], src)
            return grouped

        def quantise_tiles(name, grouped, first, count, in_ring):
            codes = staged_tile(in_ring, [P, count * P], U32, "%s_codes%d" % (name, first))
            plane = staged_tile(in_ring, [P, count * P], U8, "%s_plane%d" % (name, first))
            nc.vector.quantize_mx(codes[:].bitcast(FP8X4), plane[:], grouped[:, PACK * P * first : PACK * P * (first + count)])
            return [(codes[:, i * P : (i + 1) * P], plane[:, i * P : (i + 1) * P]) for i in range(count)]

        def product(lhs, rhs, width):
            acc = psum.tile([P, BANK], F32, name="acc")
            for part in pieces(width, (512, 256, 128)):
                nc.tensor.matmul_mx(
                    acc[:, part], lhsT=lhs[0].bitcast(FP8X4), lhsT_scale=lhs[1],
                    rhs=rhs[0][:, part].bitcast(FP8X4), rhs_scale=rhs[1][:, part], start=True, stop=True)
            return acc

        def window(name, t, acc, engine):
            tile = keep.tile([P, WINDOW], F32, name="%s%d" % (name, t))
            if engine == "scalar":
                nc.scalar.activation(tile[:, :S], acc[:], COPY, scale=root[t][:])
            else:
                nc.vector.tensor_scalar(tile[:, :S], acc[:], root[t][:], None, MULT)
            return tile

        def fetch(tile, offsets, width, sign):
            part = ring_tile([P, width], F32, "part")
            nc.scalar.activation(part[:], tile[:].indirect(offsets), COPY, scale=sign)
            return part

        root_column(0, True)
        root_column(1, True)
        x_codes = pick("x_codes", xw, U32, offs_t, False)
        x_plane = pick("x_plane", xs, U8, offs_t, False)
        w1_grouped = quantise_dealt("w1", w1_raw, (("scalar", 0, 64), ("vector", 64, 104), ("scalar", 104, 128)))
        w1q = quantise_tiles("w1", w1_grouped, 0, 1, False) + quantise_tiles("w1", w1_grouped, 1, 3, False)
        y_acc = [product(w1q[t], (x_codes, x_plane), S) for t in range(PACK)]
        w2_grouped = quantise_dealt("w2", w2_raw, (("vector", 0, 64), ("vector", 64, 128)))
        w2q = quantise_tiles("w2", w2_grouped, 0, 1, False)
        e_plane = pick("e_plane", es, U8, doc_t, False)
        e_codes = pick("e_codes", ew, U32, doc_t, False)
        w2q = w2q + quantise_tiles("w2", w2_grouped, 1, 3, False)
        e_acc = [product(w2q[t], (e_codes, e_plane), S) for t in range(PACK)]

        w3_grouped = keep.tile([P, PACK * N], BF16, name="w3_grouped", tag="pairs", align_bytes=64)
        w3_codes = keep.tile([P, N], U32, name="w3_codes", align_bytes=64)
        w3_plane = keep.tile([P, N], U8, name="w3_plane", align_bytes=64)
        nc.vector.tensor_tensor(
            w3_grouped[:].rearrange("p (c i j) -> p c j i", i=4, j=PACK),
            w3_raw[:].rearrange("p j (c i) -> p c j i", i=4),
            flip[:].unsqueeze(1).unsqueeze(3).to_broadcast([P, N // 4, PACK, 4]), MULT)
        nc.vector.quantize_mx(w3_codes[:].bitcast(FP8X4), w3_plane[:], w3_grouped[:])

        pairs = keep.tile([P, 2, PACK, U], F32, name="pairs", tag="pairs", align_bytes=64)
        pair = [pairs[:, s] for s in range(2)]
        sides = ((qb_t, db_t, -1.0), (qa_t, da_t, 1.0))
        y_engine = ("scalar", "scalar", "scalar", "scalar")
        y = {0: window("y", 0, y_acc[0], y_engine[0])}
        e = {}
        first_part = fetch(y[0], qb_t[:], U, -1.0)
        root_column(2, True)
        root_column(3, False)
        for t in range(PACK - 1):
            e[t] = window("e", t, e_acc[t], "scalar")

            for s, (q_list, d_list, sign) in enumerate(sides):
                y_part = first_part if (t, s) == (0, 0) else fetch(y[t], q_list[:], U, sign)
                nc.vector.tensor_tensor(pair[s][:, t, :], e[t][:].indirect(d_list[:]), y_part[:], ADD)
            y[t + 1] = window("y", t + 1, y_acc[t + 1], y_engine[t + 1])

        last = PACK - 1
        e[last] = window("e", last, e_acc[last], "scalar")
        start = 0
        for c, width in enumerate(CHUNKS):
            cols = slice(start // 16, (start + width) // 16)
            span = slice(start, start + width)
            for s, (q_list, d_list, sign) in enumerate(sides):
                y_part = fetch(y[last], q_list[:, cols], width, sign)
                if (c, s) in BOTH_ON_SCALAR:
                    e_part = fetch(e[last], d_list[:, cols], width, 1.0)
                    nc.vector.tensor_tensor(pair[s][:, last, span], e_part[:], y_part[:], ADD)
                else:
                    nc.vector.tensor_tensor(pair[s][:, last, span], e[last][:].indirect(d_list[:, cols]), y_part[:], ADD)
            hid = keep.tile([P, PACK * width], BF16, name="hid%d" % c, align_bytes=64)
            nc.vector.tensor_tensor(
                hid[:].rearrange("p (c i t) -> p c t i", i=4, t=PACK),
                pair[0][:, :, span].rearrange("p t (c i) -> p c t i", i=4),
                pair[1][:, :, span].rearrange("p t (c i) -> p c t i", i=4), MULT)
            hid_codes = keep.tile([P, width], U32, name="hid_codes%d" % c, align_bytes=64)
            hid_plane = keep.tile([P, width], U8, name="hid_plane%d" % c, align_bytes=64)
            nc.vector.quantize_mx(hid_codes[:].bitcast(FP8X4), hid_plane[:], hid[:])
            for h in range(N // P):
                staged = keep.tile([P, width], F32, name="staged%d_%d" % (c, h))
                rows = slice(h * P, (h + 1) * P)
                acc = product((w3_codes[:, rows], w3_plane[:, rows]), (hid_codes, hid_plane), width)
                if c == len(CHUNKS) - 1 and h == 1:
                    nc.vector.tensor_copy(staged[:], acc[:, :width])
                else:
                    nc.scalar.copy(staged[:], acc[:, :width])
                nc.sync.dma_start(out[rows, span], staged[:])
            start += width
